import numpy as np
CORES = [97,101,225,229,353,357,481,485]
N = 8
B, S = 16, 32
def entries(a): return a.T.reshape(-1)
def pack(v, P): return np.ascontiguousarray(np.asarray(v, np.int32).reshape(-1, P).T)
def lists(rng, how):
    Q = rng.integers(0, N * B, N * B)
    if how == "alike": Q[:] = rng.integers(N * B)
    if how == "stay": Q = np.arange(N * B)
    if how == "distinct": Q = rng.permutation(N * B)
    if how == "hotrank": Q = B * int(rng.integers(N)) + rng.integers(0, B, N * B)
    if how == "swap": s = int(rng.integers(1, N)); Q = np.concatenate([B * ((r + s) % N) + rng.permutation(B) for r in range(N)])
    return {"parent": np.broadcast_to(pack(Q, 16), (N, 16, N * B // 16)).copy()}
def setup_inputs(rng):
    return dict({"c": rng.standard_normal((N, 128, B * S), dtype=np.float32)}, **lists(rng, "uniform"))
def setup_inputs_alike(rng):
    d = setup_inputs(rng); d.update(lists(rng, "alike"))
    for k in ("c",): d[k] = (d[k].astype(np.float32) * 1048576.0).astype(d[k].dtype)
    return d
def setup_inputs_distinct(rng):
    d = setup_inputs(rng); d.update(lists(rng, "distinct"))
    for k in ("c",): d[k] = (d[k].astype(np.float32) * (1 / 1024.0)).astype(d[k].dtype)
    return d
def setup_inputs_hotrank(rng):
    d = setup_inputs(rng); d.update(lists(rng, "hotrank"))
    return d
def setup_inputs_stay(rng):
    d = setup_inputs(rng); d.update(lists(rng, "stay"))
    return d
def setup_inputs_swap(rng):
    d = setup_inputs(rng); d.update(lists(rng, "swap"))
    return d
def check_inputs(x):
    bad = []
    if x["parent"].min() < 0 or x["parent"].max() >= N * B: bad.append("parent out of range")
    if not all(np.array_equal(a, x["parent"][0]) for a in x["parent"]): bad.append("parent isn't alike on all ranks")
    return bad
def reference(c, parent):
    A = np.concatenate(list(c), axis=1).reshape(128, N * B, S)
    Y = A[:, entries(parent[0]), :]
    return {"y": np.stack([Y[:, B * r:B * r + B].reshape(128, B * S) for r in range(N)])}

@@ -1,0 +1,102 @@
+from concourse.bass import DstId, RemoteDMATransfer
+from concourse.mybir import AluOpType
+
+N, B, S = 8, 16, 32
+W = B * S
+G = 16
+Q = W // G
+
+SCRATCH = {
+    "win": ("sbuf", [128, N * W], "float32"),
+    "outb": ("sbuf", [128, W], "float32"),
+    "prow": ("sbuf", [1, N * B], "int32"),
+    "row": ("sbuf", [1, Q], "float32"),
+    "ones": ("sbuf", [1, 128], "float32"),
+    "m16": ("sbuf", [1, 128], "float32"),
+    "off": ("sbuf", [128, Q], "uint16"),
+    "ps": ("psum", [128, Q], "float32"),
+}
+SEMAPHORES = ["ldc", "ldp", "a1", "a2", "fin", "loc", "one", "iot", "row", "mm", "off", "sel", "st"]
+
+CABLE_FIRST = True
+
+
+def _bits(m):
+    return bin(m).count("1")
+
+
+def _peers(core, T, topo):
+    def on_chip(a, b):
+        return topo.host(a) == topo.host(b) and topo.chip(a) == topo.chip(b)
+    others = [c for c in T.cores if c != core]
+    partner = [c for c in others if on_chip(c, core)][0]
+    plane = [c for c in others if not on_chip(c, core) and topo.die(c) == topo.die(core) and topo.may_write(core, c)]
+    near = [c for c in plane if topo.same_plane(core, c)][0]
+    far = [c for c in plane if not topo.same_plane(core, c)][0]
+    return partner, near, far
+
+
+def rank_program(g, core, T, topo):
+    rank = T.rank_of(core)
+    if rank is None:
+        return
+    sem = T.sem
+    v, te = g.vector, g.tensor
+
+    partner, near, far = _peers(core, T, topo)
+    n1, n2 = (far, near) if CABLE_FIRST else (near, far)
+    n1_other = _peers(n1, T, topo)[0]
+    m_off = topo.mask(core, n1) & topo.mask(core, n2) & topo.mask(core, n1_other)
+    m_on = topo.mask(core, partner) & ~m_off
+    e_off, e_on = _bits(m_off), _bits(m_on)
+
+    def blk(c):
+        r = T.rank_of(c)
+        return T.win[:, r * W:(r + 1) * W]
+
+    def tr(src_core, dst, mask, rsem):
+        rid, pid = topo.addr(dst, core)
+        return RemoteDMATransfer(dst_ids=[DstId(rid=rid, pnc=pid)], dma_engine_mask=mask, remote_sem=rsem,
+                                 src=blk(src_core), dst=blk(src_core))
+
+    g.sync.dma_start(blk(core), T.c[:, :]).then_inc(sem.ldc, 16)
+    g.scalar.dma_start(T.prow[0:1, :], T.parent[:, :]).then_inc(sem.ldp, 16)
+
+    v.memset(T.ones[0:1, :], 1.0).then_inc(sem.one, 1)
+    g.iota(T.m16[0:1, :], [[0, 128 // G], [1, G]], 0, 0, allow_small_or_imprecise_dtypes=True).then_inc(sem.iot, 1)
+    te.wait_ge(sem.one, 1)
+    te.wait_ge(sem.iot, 1)
+    te.matmul(T.ps[:, :], T.m16[0:1, :], T.ones[0:1, 0:Q], True, False)
+    v.wait_ge(sem.ldp, 16)
+    mine = T.prow[0:1, rank:N * B:N]
+    v.tensor_scalar(T.row[0:1, 0:Q:2], mine, float(S), None, AluOpType.mult).then_inc(sem.row, 1)
+    v.tensor_scalar(T.row[0:1, 1:Q:2], mine, float(S), float(G), AluOpType.mult, AluOpType.add).then_inc(sem.row, 1)
+    te.wait_ge(sem.row, 2)
+    te.matmul(T.ps[:, :], T.ones[0:1, :], T.row[0:1, :], False, True).then_inc(sem.mm, 1)
+    v.wait_ge(sem.mm, 1)
+    v.tensor_copy(T.off[:, :], T.ps[:, :]).then_inc(sem.off, 1)
+
+    sent = 0
+    g.wait_ge(sem.ldc, 16)
+    g.remote_dma_fused([tr(core, n1, m_off, sem.a1)], local_sem=sem.loc)
+    g.remote_dma_fused([tr(core, n2, m_off, sem.a2)], local_sem=sem.loc)
+    g.remote_dma_fused([tr(core, partner, m_on, sem.fin)], local_sem=sem.loc)
+    sent += 2 * e_off + e_on
+    g.wait_ge(sem.a1, e_off)
+    g.remote_dma_fused([tr(n1, n2, m_off, sem.fin), tr(n1, partner, m_on, sem.fin)], local_sem=sem.loc)
+    sent += e_off + e_on
+    g.wait_ge(sem.a2, e_off)
+    g.remote_dma_fused([tr(n2, n1_other, m_off, sem.fin), tr(n2, partner, m_on, sem.fin)], local_sem=sem.loc)
+    sent += e_off + e_on
+
+    v.wait_ge(sem.off, 1)
+    v.wait_ge(sem.ldc, 16)
+    v.wait_ge(sem.a1, e_off)
+    v.wait_ge(sem.a2, e_off)
+    v.wait_ge(sem.fin, 3 * e_on + 2 * e_off)
+    v.tensor_copy(T.outb[:, :], T.win[:, :].indirect(T.off[:, :])).then_inc(sem.sel, 1)
+    g.sync.wait_ge(sem.sel, 1)
+    g.sync.dma_start(T.y[:, :], T.outb[:, :]).then_inc(sem.st, 16)
+
+    g.wait_ge(sem.loc, sent)
+    g.wait_ge(sem.st, 16)

@@ -5,6 +5,8 @@ N, B, S = 8, 16, 32
 W = B * S
 G = 16
 Q = W // G
+CH = 2
+CW = W // CH
 
 SCRATCH = {
     "win": ("sbuf", [128, N * W], "float32"),
@@ -16,13 +18,17 @@ SCRATCH = {
     "off": ("sbuf", [128, Q], "uint16"),
     "ps": ("psum", [128, Q], "float32"),
 }
-SEMAPHORES = ["ldc", "ldp", "a1", "a2", "fin", "loc", "one", "iot", "row", "mm", "off", "sel", "st"]
-
-CABLE_FIRST = True
+SEMAPHORES = (["ldp", "fin", "loc", "one", "iot", "row", "mm", "off", "sel", "st"]
+              + ["ld%d" % k for k in range(CH)] + ["a1_%d" % k for k in range(CH)] + ["a2_%d" % k for k in range(CH)])
 
 
 def _bits(m):
     return bin(m).count("1")
+
+
+def _alternate(m):
+    bits = [i for i in range(m.bit_length()) if (m >> i) & 1]
+    return sum(1 << i for i in bits[0::2]), sum(1 << i for i in bits[1::2])
 
 
 def _peers(core, T, topo):
@@ -43,23 +49,25 @@ def rank_program(g, core, T, topo):
     sem = T.sem
     v, te = g.vector, g.tensor
 
-    partner, near, far = _peers(core, T, topo)
-    n1, n2 = (far, near) if CABLE_FIRST else (near, far)
+    partner, n2, n1 = _peers(core, T, topo)
     n1_other = _peers(n1, T, topo)[0]
     m_off = topo.mask(core, n1) & topo.mask(core, n2) & topo.mask(core, n1_other)
     m_on = topo.mask(core, partner) & ~m_off
-    e_off, e_on = _bits(m_off), _bits(m_on)
+    m_1, m_2 = _alternate(m_off)
+    e_1, e_2, e_on = _bits(m_1), _bits(m_2), _bits(m_on)
 
-    def blk(c):
-        r = T.rank_of(c)
-        return T.win[:, r * W:(r + 1) * W]
+    def blk(c, k=None):
+        a = T.rank_of(c) * W
+        return T.win[:, a:a + W] if k is None else T.win[:, a + k * CW:a + (k + 1) * CW]
 
-    def tr(src_core, dst, mask, rsem):
+    def tr(src_core, k, dst, mask, rsem):
         rid, pid = topo.addr(dst, core)
         return RemoteDMATransfer(dst_ids=[DstId(rid=rid, pnc=pid)], dma_engine_mask=mask, remote_sem=rsem,
-                                 src=blk(src_core), dst=blk(src_core))
+                                 src=blk(src_core, k), dst=blk(src_core, k))
 
-    g.sync.dma_start(blk(core), T.c[:, :]).then_inc(sem.ldc, 16)
+    for k in range(CH):
+        q = g.sync if k % 2 == 0 else g.scalar
+        q.dma_start(blk(core, k), T.c[:, k * CW:(k + 1) * CW]).then_inc(sem["ld%d" % k], 16)
     g.scalar.dma_start(T.prow[0:1, :], T.parent[:, :]).then_inc(sem.ldp, 16)
 
     v.memset(T.ones[0:1, :], 1.0).then_inc(sem.one, 1)
@@ -77,23 +85,26 @@ def rank_program(g, core, T, topo):
     v.tensor_copy(T.off[:, :], T.ps[:, :]).then_inc(sem.off, 1)
 
     sent = 0
-    g.wait_ge(sem.ldc, 16)
-    g.remote_dma_fused([tr(core, n1, m_off, sem.a1)], local_sem=sem.loc)
-    g.remote_dma_fused([tr(core, n2, m_off, sem.a2)], local_sem=sem.loc)
-    g.remote_dma_fused([tr(core, partner, m_on, sem.fin)], local_sem=sem.loc)
-    sent += 2 * e_off + e_on
-    g.wait_ge(sem.a1, e_off)
-    g.remote_dma_fused([tr(n1, n2, m_off, sem.fin), tr(n1, partner, m_on, sem.fin)], local_sem=sem.loc)
-    sent += e_off + e_on
-    g.wait_ge(sem.a2, e_off)
-    g.remote_dma_fused([tr(n2, n1_other, m_off, sem.fin), tr(n2, partner, m_on, sem.fin)], local_sem=sem.loc)
-    sent += e_off + e_on
+    for k in range(CH):
+        g.wait_ge(sem["ld%d" % k], 16)
+        g.remote_dma_fused([tr(core, k, n1, m_1, sem["a1_%d" % k]), tr(core, k, n2, m_2, sem["a2_%d" % k])],
+                           local_sem=sem.loc)
+        sent += e_1 + e_2
+    g.remote_dma_fused([tr(core, None, partner, m_on, sem.fin)], local_sem=sem.loc)
+    sent += e_on
+    for k in range(CH):
+        g.wait_ge(sem["a1_%d" % k], e_1)
+        g.remote_dma_fused([tr(n1, k, n2, m_2, sem.fin), tr(n1, k, partner, m_on, sem.fin)], local_sem=sem.loc)
+        g.wait_ge(sem["a2_%d" % k], e_2)
+        g.remote_dma_fused([tr(n2, k, n1_other, m_1, sem.fin), tr(n2, k, partner, m_on, sem.fin)], local_sem=sem.loc)
+        sent += e_1 + e_2 + 2 * e_on
 
     v.wait_ge(sem.off, 1)
-    v.wait_ge(sem.ldc, 16)
-    v.wait_ge(sem.a1, e_off)
-    v.wait_ge(sem.a2, e_off)
-    v.wait_ge(sem.fin, 3 * e_on + 2 * e_off)
+    for k in range(CH):
+        v.wait_ge(sem["ld%d" % k], 16)
+        v.wait_ge(sem["a1_%d" % k], e_1)
+        v.wait_ge(sem["a2_%d" % k], e_2)
+    v.wait_ge(sem.fin, e_on + 2 * CH * e_on + CH * (e_1 + e_2))
     v.tensor_copy(T.outb[:, :], T.win[:, :].indirect(T.off[:, :])).then_inc(sem.sel, 1)
     g.sync.wait_ge(sem.sel, 1)
     g.sync.dma_start(T.y[:, :], T.outb[:, :]).then_inc(sem.st, 16)

@@ -18,8 +18,8 @@ SCRATCH = {
     "off": ("sbuf", [128, Q], "uint16"),
     "ps": ("psum", [128, Q], "float32"),
 }
-SEMAPHORES = (["ldp", "fin", "loc", "one", "iot", "row", "mm", "off", "sel", "st"]
-              + ["ld%d" % k for k in range(CH)] + ["a1_%d" % k for k in range(CH)] + ["a2_%d" % k for k in range(CH)])
+SEMAPHORES = (["ldp", "a2", "fin", "loc", "one", "iot", "row", "mm", "off", "sel", "st"]
+              + ["ld%d" % k for k in range(CH)] + ["a1_%d" % k for k in range(CH)])
 
 
 def _bits(m):
@@ -50,8 +50,8 @@ def rank_program(g, core, T, topo):
     v, te = g.vector, g.tensor
 
     partner, n2, n1 = _peers(core, T, topo)
-    n1_other = _peers(n1, T, topo)[0]
-    m_off = topo.mask(core, n1) & topo.mask(core, n2) & topo.mask(core, n1_other)
+    n2_other = _peers(n2, T, topo)[0]
+    m_off = topo.mask(core, n1) & topo.mask(core, n2) & topo.mask(core, n2_other)
     m_on = topo.mask(core, partner) & ~m_off
     m_1, m_2 = _alternate(m_off)
     e_1, e_2, e_on = _bits(m_1), _bits(m_2), _bits(m_on)
@@ -87,24 +87,26 @@ def rank_program(g, core, T, topo):
     sent = 0
     for k in range(CH):
         g.wait_ge(sem["ld%d" % k], 16)
-        g.remote_dma_fused([tr(core, k, n1, m_1, sem["a1_%d" % k]), tr(core, k, n2, m_2, sem["a2_%d" % k])],
-                           local_sem=sem.loc)
-        sent += e_1 + e_2
-    g.remote_dma_fused([tr(core, None, partner, m_on, sem.fin)], local_sem=sem.loc)
-    sent += e_on
+        g.remote_dma_fused([tr(core, k, n1, m_1, sem["a1_%d" % k])], local_sem=sem.loc)
+        sent += e_1
+    g.remote_dma_fused([tr(core, None, n2, m_2, sem.a2), tr(core, None, partner, m_on, sem.fin)], local_sem=sem.loc)
+    sent += e_2 + e_on
     for k in range(CH):
         g.wait_ge(sem["a1_%d" % k], e_1)
-        g.remote_dma_fused([tr(n1, k, n2, m_2, sem.fin), tr(n1, k, partner, m_on, sem.fin)], local_sem=sem.loc)
-        g.wait_ge(sem["a2_%d" % k], e_2)
-        g.remote_dma_fused([tr(n2, k, n1_other, m_1, sem.fin), tr(n2, k, partner, m_on, sem.fin)], local_sem=sem.loc)
-        sent += e_1 + e_2 + 2 * e_on
+        g.remote_dma_fused([tr(n1, k, n2, m_2, sem.fin), tr(n1, k, n2_other, m_1, sem.fin),
+                            tr(n1, k, partner, m_on, sem.fin)], local_sem=sem.loc)
+        sent += e_1 + e_2 + e_on
+        if k == 0:
+            g.wait_ge(sem.a2, e_2)
+            g.remote_dma_fused([tr(n2, None, partner, m_on, sem.fin)], local_sem=sem.loc)
+            sent += e_on
 
     v.wait_ge(sem.off, 1)
     for k in range(CH):
         v.wait_ge(sem["ld%d" % k], 16)
         v.wait_ge(sem["a1_%d" % k], e_1)
-        v.wait_ge(sem["a2_%d" % k], e_2)
-    v.wait_ge(sem.fin, e_on + 2 * CH * e_on + CH * (e_1 + e_2))
+    v.wait_ge(sem.a2, e_2)
+    v.wait_ge(sem.fin, 2 * e_on + CH * (e_on + e_1 + e_2))
     v.tensor_copy(T.outb[:, :], T.win[:, :].indirect(T.off[:, :])).then_inc(sem.sel, 1)
     g.sync.wait_ge(sem.sel, 1)
     g.sync.dma_start(T.y[:, :], T.outb[:, :]).then_inc(sem.st, 16)

@@ -5,8 +5,10 @@ N, B, S = 8, 16, 32
 W = B * S
 G = 16
 Q = W // G
-CH = 2
-CW = W // CH
+SIM = 512
+PIECES = [(0, W // 2), (W // 2, 3 * W // 4), (3 * W // 4, W)]
+NP = len(PIECES)
+HP = NP - 1
 
 SCRATCH = {
     "win": ("sbuf", [128, N * W], "float32"),
@@ -18,8 +20,8 @@ SCRATCH = {
     "off": ("sbuf", [128, Q], "uint16"),
     "ps": ("psum", [128, Q], "float32"),
 }
-SEMAPHORES = (["ldp", "a2", "fin", "loc", "one", "iot", "row", "mm", "off", "sel", "st"]
-              + ["ld%d" % k for k in range(CH)] + ["a1_%d" % k for k in range(CH)])
+SEMAPHORES = (["ldp", "a2", "fin", "loc", "one", "iot", "row", "mm", "off", "sel", "st", "hin"]
+              + ["ld%d" % k for k in range(NP)] + ["a1_%d" % k for k in range(NP)])
 
 
 def _bits(m):
@@ -31,43 +33,65 @@ def _alternate(m):
     return sum(1 << i for i in bits[0::2]), sum(1 << i for i in bits[1::2])
 
 
+def _on_chip(a, b, topo):
+    return topo.host(a) == topo.host(b) and topo.chip(a) == topo.chip(b)
+
+
 def _peers(core, T, topo):
-    def on_chip(a, b):
-        return topo.host(a) == topo.host(b) and topo.chip(a) == topo.chip(b)
     others = [c for c in T.cores if c != core]
-    partner = [c for c in others if on_chip(c, core)][0]
-    plane = [c for c in others if not on_chip(c, core) and topo.die(c) == topo.die(core) and topo.may_write(core, c)]
+    partner = [c for c in others if _on_chip(c, core, topo)][0]
+    plane = [c for c in others if not _on_chip(c, core, topo) and topo.die(c) == topo.die(core) and topo.may_write(core, c)]
     near = [c for c in plane if topo.same_plane(core, c)][0]
     far = [c for c in plane if not topo.same_plane(core, c)][0]
     return partner, near, far
 
 
-def rank_program(g, core, T, topo):
-    rank = T.rank_of(core)
-    if rank is None:
-        return
-    sem = T.sem
-    v, te = g.vector, g.tensor
+def _helper(r, T, topo):
+    mate = [x for x in range(SIM) if topo.mates(r, x)][0]
+    return [x for x in range(SIM) if _on_chip(x, r, topo) and topo.die(x) == topo.die(r) and x not in T.cores
+            and topo.may_write(x, mate) != topo.may_write(r, mate)][0]
 
-    partner, n2, n1 = _peers(core, T, topo)
-    n2_other = _peers(n2, T, topo)[0]
-    m_off = topo.mask(core, n1) & topo.mask(core, n2) & topo.mask(core, n2_other)
-    m_on = topo.mask(core, partner) & ~m_off
-    m_1, m_2 = _alternate(m_off)
-    e_1, e_2, e_on = _bits(m_1), _bits(m_2), _bits(m_on)
+
+def rank_program(g, core, T, topo):
+    sem = T.sem
 
     def blk(c, k=None):
         a = T.rank_of(c) * W
-        return T.win[:, a:a + W] if k is None else T.win[:, a + k * CW:a + (k + 1) * CW]
+        return T.win[:, a:a + W] if k is None else T.win[:, a + PIECES[k][0]:a + PIECES[k][1]]
 
     def tr(src_core, k, dst, mask, rsem):
         rid, pid = topo.addr(dst, core)
         return RemoteDMATransfer(dst_ids=[DstId(rid=rid, pnc=pid)], dma_engine_mask=mask, remote_sem=rsem,
                                  src=blk(src_core, k), dst=blk(src_core, k))
 
-    for k in range(CH):
-        q = g.sync if k % 2 == 0 else g.scalar
-        q.dma_start(blk(core, k), T.c[:, k * CW:(k + 1) * CW]).then_inc(sem["ld%d" % k], 16)
+    rank = T.rank_of(core)
+    if rank is None:
+        mine = [r for r in T.cores if _on_chip(r, core, topo) and _helper(r, T, topo) == core]
+        if not mine:
+            return
+        r = mine[0]
+        far = _peers(r, T, topo)[2]
+        m_in = topo.mask(r, core) & ~topo.mask(r, far)
+        m_h = topo.mask(core, far)
+        g.wait_ge(sem.hin, _bits(m_in))
+        g.remote_dma_fused([tr(r, HP, far, m_h, sem["a1_%d" % HP])], local_sem=sem.loc)
+        g.wait_ge(sem.loc, _bits(m_h))
+        return
+
+    v, te = g.vector, g.tensor
+    partner, n2, n1 = _peers(core, T, topo)
+    n2_other = _peers(n2, T, topo)[0]
+    helper = _helper(core, T, topo)
+    m_off = topo.mask(core, n1) & topo.mask(core, n2) & topo.mask(core, n2_other)
+    m_on = topo.mask(core, partner) & topo.mask(core, helper) & ~m_off
+    m_1, m_2 = _alternate(m_off)
+    e_1, e_2, e_on = _bits(m_1), _bits(m_2), _bits(m_on)
+    e_in = [e_1] * HP + [_bits(topo.mask(_helper(n1, T, topo), core))]
+
+    g.sync.dma_start(blk(core, 0), T.c[:, PIECES[0][0]:PIECES[0][1]]).then_inc(sem.ld0, 16)
+    g.scalar.dma_start(blk(core, HP), T.c[:, PIECES[HP][0]:PIECES[HP][1]]).then_inc(sem["ld%d" % HP], 16)
+    for k in range(1, HP):
+        g.sync.dma_start(blk(core, k), T.c[:, PIECES[k][0]:PIECES[k][1]]).then_inc(sem["ld%d" % k], 16)
     g.scalar.dma_start(T.prow[0:1, :], T.parent[:, :]).then_inc(sem.ldp, 16)
 
     v.memset(T.ones[0:1, :], 1.0).then_inc(sem.one, 1)
@@ -85,14 +109,19 @@ def rank_program(g, core, T, topo):
     v.tensor_copy(T.off[:, :], T.ps[:, :]).then_inc(sem.off, 1)
 
     sent = 0
-    for k in range(CH):
+    g.wait_ge(sem.ld0, 16)
+    g.remote_dma_fused([tr(core, 0, n1, m_1, sem.a1_0)], local_sem=sem.loc)
+    g.wait_ge(sem["ld%d" % HP], 16)
+    g.remote_dma_fused([tr(core, HP, helper, m_on, sem.hin)], local_sem=sem.loc)
+    sent += e_1 + e_on
+    for k in range(1, HP):
         g.wait_ge(sem["ld%d" % k], 16)
         g.remote_dma_fused([tr(core, k, n1, m_1, sem["a1_%d" % k])], local_sem=sem.loc)
         sent += e_1
     g.remote_dma_fused([tr(core, None, n2, m_2, sem.a2), tr(core, None, partner, m_on, sem.fin)], local_sem=sem.loc)
     sent += e_2 + e_on
-    for k in range(CH):
-        g.wait_ge(sem["a1_%d" % k], e_1)
+    for k in range(NP):
+        g.wait_ge(sem["a1_%d" % k], e_in[k])
         g.remote_dma_fused([tr(n1, k, n2, m_2, sem.fin), tr(n1, k, n2_other, m_1, sem.fin),
                             tr(n1, k, partner, m_on, sem.fin)], local_sem=sem.loc)
         sent += e_1 + e_2 + e_on
@@ -102,11 +131,11 @@ def rank_program(g, core, T, topo):
             sent += e_on
 
     v.wait_ge(sem.off, 1)
-    for k in range(CH):
+    for k in range(NP):
         v.wait_ge(sem["ld%d" % k], 16)
-        v.wait_ge(sem["a1_%d" % k], e_1)
+        v.wait_ge(sem["a1_%d" % k], e_in[k])
     v.wait_ge(sem.a2, e_2)
-    v.wait_ge(sem.fin, 2 * e_on + CH * (e_on + e_1 + e_2))
+    v.wait_ge(sem.fin, 2 * e_on + NP * (e_on + e_1 + e_2))
     v.tensor_copy(T.outb[:, :], T.win[:, :].indirect(T.off[:, :])).then_inc(sem.sel, 1)
     g.sync.wait_ge(sem.sel, 1)
     g.sync.dma_start(T.y[:, :], T.outb[:, :]).then_inc(sem.st, 16)

@@ -6,7 +6,7 @@ W = B * S
 G = 16
 Q = W // G
 SIM = 512
-PIECES = [(0, W // 2), (W // 2, 3 * W // 4), (3 * W // 4, W)]
+PIECES = [(0, 3 * W // 8), (3 * W // 8, 5 * W // 8), (5 * W // 8, W)]
 NP = len(PIECES)
 HP = NP - 1
 

@@ -6,9 +6,10 @@ W = B * S
 G = 16
 Q = W // G
 SIM = 512
-PIECES = [(0, 3 * W // 8), (3 * W // 8, 5 * W // 8), (5 * W // 8, W)]
+CUTS = [0, 5 * W // 16, 9 * W // 16, 13 * W // 16, W]
+PIECES = [(CUTS[k], CUTS[k + 1]) for k in range(len(CUTS) - 1)]
 NP = len(PIECES)
-HP = NP - 1
+HP = 2
 
 SCRATCH = {
     "win": ("sbuf", [128, N * W], "float32"),
@@ -20,8 +21,9 @@ SCRATCH = {
     "off": ("sbuf", [128, Q], "uint16"),
     "ps": ("psum", [128, Q], "float32"),
 }
-SEMAPHORES = (["ldp", "a2", "fin", "loc", "one", "iot", "row", "mm", "off", "sel", "st", "hin"]
-              + ["ld%d" % k for k in range(NP)] + ["a1_%d" % k for k in range(NP)])
+SEMAPHORES = (["ldp", "a2", "fin", "loc", "one", "iot", "row", "mm", "off", "sel", "st"]
+              + ["ld%d" % k for k in range(NP)] + ["a1_%d" % k for k in range(HP)]
+              + ["hin%d" % k for k in range(HP, NP)] + ["hx%d" % k for k in range(HP, NP)])
 
 
 def _bits(m):
@@ -52,6 +54,14 @@ def _helper(r, T, topo):
             and topo.may_write(x, mate) != topo.may_write(r, mate)][0]
 
 
+def _helper_masks(h, r, T, topo):
+    partner, n2, n1 = _peers(r, T, topo)
+    off = topo.mask(h, _helper(n1, T, topo)) & topo.mask(h, n2) & topo.mask(h, _peers(n2, T, topo)[0])
+    m_a, m_b = _alternate(off)
+    on = _alternate(topo.mask(h, r) & topo.mask(h, partner) & ~off)
+    return m_a, {k: ((m_a, m_b) if k == NP - 1 else _alternate(m_b)) + on for k in range(HP, NP)}
+
+
 def rank_program(g, core, T, topo):
     sem = T.sem
 
@@ -70,12 +80,22 @@ def rank_program(g, core, T, topo):
         if not mine:
             return
         r = mine[0]
-        far = _peers(r, T, topo)[2]
-        m_in = topo.mask(r, core) & ~topo.mask(r, far)
-        m_h = topo.mask(core, far)
-        g.wait_ge(sem.hin, _bits(m_in))
-        g.remote_dma_fused([tr(r, HP, far, m_h, sem["a1_%d" % HP])], local_sem=sem.loc)
-        g.wait_ge(sem.loc, _bits(m_h))
+        partner, n2, n1 = _peers(r, T, topo)
+        n2_other = _peers(n2, T, topo)[0]
+        hfar = _helper(n1, T, topo)
+        m_in = topo.mask(r, core) & ~topo.mask(r, n1)
+        m_cab, m_sp = _helper_masks(core, r, T, topo)
+        sent = 0
+        for k in range(HP, NP):
+            g.wait_ge(sem["hin%d" % k], _bits(m_in))
+            g.remote_dma_fused([tr(r, k, hfar, m_cab, sem["hx%d" % k])], local_sem=sem.loc)
+            sent += _bits(m_cab)
+        for k in range(HP, NP):
+            g.wait_ge(sem["hx%d" % k], _bits(m_cab))
+            g.remote_dma_fused([tr(n1, k, n2, m_sp[k][0], sem.fin), tr(n1, k, n2_other, m_sp[k][1], sem.fin)], local_sem=sem.loc)
+            g.remote_dma_fused([tr(n1, k, r, m_sp[k][2], sem.fin), tr(n1, k, partner, m_sp[k][3], sem.fin)], local_sem=sem.loc)
+            sent += sum(_bits(m) for m in m_sp[k])
+        g.wait_ge(sem.loc, sent)
         return
 
     v, te = g.vector, g.tensor
@@ -86,10 +106,11 @@ def rank_program(g, core, T, topo):
     m_on = topo.mask(core, partner) & topo.mask(core, helper) & ~m_off
     m_1, m_2 = _alternate(m_off)
     e_1, e_2, e_on = _bits(m_1), _bits(m_2), _bits(m_on)
-    e_in = [e_1] * HP + [_bits(topo.mask(_helper(n1, T, topo), core))]
+    e_h = sum(_bits(m) for ms in _helper_masks(helper, core, T, topo)[1].values() for m in ms)
 
     g.sync.dma_start(blk(core, 0), T.c[:, PIECES[0][0]:PIECES[0][1]]).then_inc(sem.ld0, 16)
-    g.scalar.dma_start(blk(core, HP), T.c[:, PIECES[HP][0]:PIECES[HP][1]]).then_inc(sem["ld%d" % HP], 16)
+    for k in range(HP, NP):
+        g.scalar.dma_start(blk(core, k), T.c[:, PIECES[k][0]:PIECES[k][1]]).then_inc(sem["ld%d" % k], 16)
     for k in range(1, HP):
         g.sync.dma_start(blk(core, k), T.c[:, PIECES[k][0]:PIECES[k][1]]).then_inc(sem["ld%d" % k], 16)
     g.scalar.dma_start(T.prow[0:1, :], T.parent[:, :]).then_inc(sem.ldp, 16)
@@ -111,17 +132,19 @@ def rank_program(g, core, T, topo):
     sent = 0
     g.wait_ge(sem.ld0, 16)
     g.remote_dma_fused([tr(core, 0, n1, m_1, sem.a1_0)], local_sem=sem.loc)
-    g.wait_ge(sem["ld%d" % HP], 16)
-    g.remote_dma_fused([tr(core, HP, helper, m_on, sem.hin)], local_sem=sem.loc)
-    sent += e_1 + e_on
+    sent += e_1
+    for k in range(HP, NP):
+        g.wait_ge(sem["ld%d" % k], 16)
+        g.remote_dma_fused([tr(core, k, helper, m_on, sem["hin%d" % k])], local_sem=sem.loc)
+        sent += e_on
     for k in range(1, HP):
         g.wait_ge(sem["ld%d" % k], 16)
         g.remote_dma_fused([tr(core, k, n1, m_1, sem["a1_%d" % k])], local_sem=sem.loc)
         sent += e_1
     g.remote_dma_fused([tr(core, None, n2, m_2, sem.a2), tr(core, None, partner, m_on, sem.fin)], local_sem=sem.loc)
     sent += e_2 + e_on
-    for k in range(NP):
-        g.wait_ge(sem["a1_%d" % k], e_in[k])
+    for k in range(HP):
+        g.wait_ge(sem["a1_%d" % k], e_1)
         g.remote_dma_fused([tr(n1, k, n2, m_2, sem.fin), tr(n1, k, n2_other, m_1, sem.fin),
                             tr(n1, k, partner, m_on, sem.fin)], local_sem=sem.loc)
         sent += e_1 + e_2 + e_on
@@ -133,9 +156,10 @@ def rank_program(g, core, T, topo):
     v.wait_ge(sem.off, 1)
     for k in range(NP):
         v.wait_ge(sem["ld%d" % k], 16)
-        v.wait_ge(sem["a1_%d" % k], e_in[k])
+    for k in range(HP):
+        v.wait_ge(sem["a1_%d" % k], e_1)
     v.wait_ge(sem.a2, e_2)
-    v.wait_ge(sem.fin, 2 * e_on + NP * (e_on + e_1 + e_2))
+    v.wait_ge(sem.fin, 2 * e_on + HP * (e_on + e_1 + e_2) + e_h)
     v.tensor_copy(T.outb[:, :], T.win[:, :].indirect(T.off[:, :])).then_inc(sem.sel, 1)
     g.sync.wait_ge(sem.sel, 1)
     g.sync.dma_start(T.y[:, :], T.outb[:, :]).then_inc(sem.st, 16)

from concourse.bass import DstId, RemoteDMATransfer
from concourse.mybir import AluOpType

N, B, S = 8, 16, 32
W = B * S
G = 16
Q = W // G
SIM = 512
CUTS = [0, 5 * W // 16, 9 * W // 16, 13 * W // 16, W]
PIECES = [(CUTS[k], CUTS[k + 1]) for k in range(len(CUTS) - 1)]
NP = len(PIECES)
HP = 2

SCRATCH = {
    "win": ("sbuf", [128, N * W], "float32"),
    "outb": ("sbuf", [128, W], "float32"),
    "prow": ("sbuf", [1, N * B], "int32"),
    "row": ("sbuf", [1, Q], "float32"),
    "ones": ("sbuf", [1, 128], "float32"),
    "m16": ("sbuf", [1, 128], "float32"),
    "off": ("sbuf", [128, Q], "uint16"),
    "ps": ("psum", [128, Q], "float32"),
}
SEMAPHORES = (["ldp", "a2", "fin", "loc", "one", "iot", "row", "mm", "off", "sel", "st"]
              + ["ld%d" % k for k in range(NP)] + ["a1_%d" % k for k in range(HP)]
              + ["hin%d" % k for k in range(HP, NP)] + ["hx%d" % k for k in range(HP, NP)])


def _bits(m):
    return bin(m).count("1")


def _alternate(m):
    bits = [i for i in range(m.bit_length()) if (m >> i) & 1]
    return sum(1 << i for i in bits[0::2]), sum(1 << i for i in bits[1::2])


def _on_chip(a, b, topo):
    return topo.host(a) == topo.host(b) and topo.chip(a) == topo.chip(b)


def _peers(core, T, topo):
    others = [c for c in T.cores if c != core]
    partner = [c for c in others if _on_chip(c, core, topo)][0]
    plane = [c for c in others if not _on_chip(c, core, topo) and topo.die(c) == topo.die(core) and topo.may_write(core, c)]
    near = [c for c in plane if topo.same_plane(core, c)][0]
    far = [c for c in plane if not topo.same_plane(core, c)][0]
    return partner, near, far


def _helper(r, T, topo):
    mate = [x for x in range(SIM) if topo.mates(r, x)][0]
    return [x for x in range(SIM) if _on_chip(x, r, topo) and topo.die(x) == topo.die(r) and x not in T.cores
            and topo.may_write(x, mate) != topo.may_write(r, mate)][0]


def _helper_masks(h, r, T, topo):
    partner, n2, n1 = _peers(r, T, topo)
    off = topo.mask(h, _helper(n1, T, topo)) & topo.mask(h, n2) & topo.mask(h, _peers(n2, T, topo)[0])
    m_a, m_b = _alternate(off)
    on = _alternate(topo.mask(h, r) & topo.mask(h, partner) & ~off)
    return m_a, {k: ((m_a, m_b) if k == NP - 1 else _alternate(m_b)) + on for k in range(HP, NP)}


def rank_program(g, core, T, topo):
    sem = T.sem

    def blk(c, k=None):
        a = T.rank_of(c) * W
        return T.win[:, a:a + W] if k is None else T.win[:, a + PIECES[k][0]:a + PIECES[k][1]]

    def tr(src_core, k, dst, mask, rsem):
        rid, pid = topo.addr(dst, core)
        return RemoteDMATransfer(dst_ids=[DstId(rid=rid, pnc=pid)], dma_engine_mask=mask, remote_sem=rsem,
                                 src=blk(src_core, k), dst=blk(src_core, k))

    rank = T.rank_of(core)
    if rank is None:
        mine = [r for r in T.cores if _on_chip(r, core, topo) and _helper(r, T, topo) == core]
        if not mine:
            return
        r = mine[0]
        partner, n2, n1 = _peers(r, T, topo)
        n2_other = _peers(n2, T, topo)[0]
        hfar = _helper(n1, T, topo)
        m_in = topo.mask(r, core) & ~topo.mask(r, n1)
        m_cab, m_sp = _helper_masks(core, r, T, topo)
        sent = 0
        for k in range(HP, NP):
            g.wait_ge(sem["hin%d" % k], _bits(m_in))
            g.remote_dma_fused([tr(r, k, hfar, m_cab, sem["hx%d" % k])], local_sem=sem.loc)
            sent += _bits(m_cab)
        for k in range(HP, NP):
            g.wait_ge(sem["hx%d" % k], _bits(m_cab))
            g.remote_dma_fused([tr(n1, k, n2, m_sp[k][0], sem.fin), tr(n1, k, n2_other, m_sp[k][1], sem.fin)], local_sem=sem.loc)
            g.remote_dma_fused([tr(n1, k, r, m_sp[k][2], sem.fin), tr(n1, k, partner, m_sp[k][3], sem.fin)], local_sem=sem.loc)
            sent += sum(_bits(m) for m in m_sp[k])
        g.wait_ge(sem.loc, sent)
        return

    v, te = g.vector, g.tensor
    partner, n2, n1 = _peers(core, T, topo)
    n2_other = _peers(n2, T, topo)[0]
    helper = _helper(core, T, topo)
    m_off = topo.mask(core, n1) & topo.mask(core, n2) & topo.mask(core, n2_other)
    m_on = topo.mask(core, partner) & topo.mask(core, helper) & ~m_off
    m_1, m_2 = _alternate(m_off)
    e_1, e_2, e_on = _bits(m_1), _bits(m_2), _bits(m_on)
    e_h = sum(_bits(m) for ms in _helper_masks(helper, core, T, topo)[1].values() for m in ms)

    g.sync.dma_start(blk(core, 0), T.c[:, PIECES[0][0]:PIECES[0][1]]).then_inc(sem.ld0, 16)
    for k in range(HP, NP):
        g.scalar.dma_start(blk(core, k), T.c[:, PIECES[k][0]:PIECES[k][1]]).then_inc(sem["ld%d" % k], 16)
    for k in range(1, HP):
        g.sync.dma_start(blk(core, k), T.c[:, PIECES[k][0]:PIECES[k][1]]).then_inc(sem["ld%d" % k], 16)
    g.scalar.dma_start(T.prow[0:1, :], T.parent[:, :]).then_inc(sem.ldp, 16)

    v.memset(T.ones[0:1, :], 1.0).then_inc(sem.one, 1)
    g.iota(T.m16[0:1, :], [[0, 128 // G], [1, G]], 0, 0, allow_small_or_imprecise_dtypes=True).then_inc(sem.iot, 1)
    te.wait_ge(sem.one, 1)
    te.wait_ge(sem.iot, 1)
    te.matmul(T.ps[:, :], T.m16[0:1, :], T.ones[0:1, 0:Q], True, False)
    v.wait_ge(sem.ldp, 16)
    mine = T.prow[0:1, rank:N * B:N]
    v.tensor_scalar(T.row[0:1, 0:Q:2], mine, float(S), None, AluOpType.mult).then_inc(sem.row, 1)
    v.tensor_scalar(T.row[0:1, 1:Q:2], mine, float(S), float(G), AluOpType.mult, AluOpType.add).then_inc(sem.row, 1)
    te.wait_ge(sem.row, 2)
    te.matmul(T.ps[:, :], T.ones[0:1, :], T.row[0:1, :], False, True).then_inc(sem.mm, 1)
    v.wait_ge(sem.mm, 1)
    v.tensor_copy(T.off[:, :], T.ps[:, :]).then_inc(sem.off, 1)

    sent = 0
    g.wait_ge(sem.ld0, 16)
    g.remote_dma_fused([tr(core, 0, n1, m_1, sem.a1_0)], local_sem=sem.loc)
    sent += e_1
    for k in range(HP, NP):
        g.wait_ge(sem["ld%d" % k], 16)
        g.remote_dma_fused([tr(core, k, helper, m_on, sem["hin%d" % k])], local_sem=sem.loc)
        sent += e_on
    for k in range(1, HP):
        g.wait_ge(sem["ld%d" % k], 16)
        g.remote_dma_fused([tr(core, k, n1, m_1, sem["a1_%d" % k])], local_sem=sem.loc)
        sent += e_1
    g.remote_dma_fused([tr(core, None, n2, m_2, sem.a2), tr(core, None, partner, m_on, sem.fin)], local_sem=sem.loc)
    sent += e_2 + e_on
    for k in range(HP):
        g.wait_ge(sem["a1_%d" % k], e_1)
        g.remote_dma_fused([tr(n1, k, n2, m_2, sem.fin), tr(n1, k, n2_other, m_1, sem.fin),
                            tr(n1, k, partner, m_on, sem.fin)], local_sem=sem.loc)
        sent += e_1 + e_2 + e_on
        if k == 0:
            g.wait_ge(sem.a2, e_2)
            g.remote_dma_fused([tr(n2, None, partner, m_on, sem.fin)], local_sem=sem.loc)
            sent += e_on

    v.wait_ge(sem.off, 1)
    for k in range(NP):
        v.wait_ge(sem["ld%d" % k], 16)
    for k in range(HP):
        v.wait_ge(sem["a1_%d" % k], e_1)
    v.wait_ge(sem.a2, e_2)
    v.wait_ge(sem.fin, 2 * e_on + HP * (e_on + e_1 + e_2) + e_h)
    v.tensor_copy(T.outb[:, :], T.win[:, :].indirect(T.off[:, :])).then_inc(sem.sel, 1)
    g.sync.wait_ge(sem.sel, 1)
    g.sync.dma_start(T.y[:, :], T.outb[:, :]).then_inc(sem.st, 16)

    g.wait_ge(sem.loc, sent)
    g.wait_ge(sem.st, 16)
